import numpy as np, ml_dtypes
CORES = [242,247,114,119]
N = 4
TK = 512
def setup_inputs(rng):
    return {"x": rng.standard_normal((N, 128, N * TK), dtype=np.float32).astype(ml_dtypes.bfloat16), "t": rng.standard_normal((N, 128, N * TK), dtype=np.float32).astype(ml_dtypes.bfloat16), "f1": (rng.standard_normal((N, 128, 128), dtype=np.float32) / 11).astype(ml_dtypes.bfloat16), "f2": (rng.standard_normal((N, 128, 128), dtype=np.float32) / 11).astype(ml_dtypes.bfloat16)}
def setup_inputs_big(rng):
    d = setup_inputs(rng)
    for k in ("x", "t", "f1", "f2"): d[k] = (d[k].astype(np.float32) * 1024.0).astype(d[k].dtype)
    return d
def setup_inputs_small(rng):
    d = setup_inputs(rng)
    for k in ("x", "t", "f1", "f2"): d[k] = (d[k].astype(np.float32) * (1 / 1024.0)).astype(d[k].dtype)
    return d
def reference(x, t, f1, f2):
    X, T, F1, F2 = x.astype(np.float64), t.astype(np.float64), f1.astype(np.float64), f2.astype(np.float64)
    y = np.zeros((N, 128, N * TK))
    for j in range(N):
        u = (F1[j].T @ X[j]) * T[j]
        for r in range(N):
            y[r][:, TK * j:TK * j + TK] = F2[r].T @ u[:, TK * r:TK * r + TK]
    return {"y": y.astype(ml_dtypes.bfloat16)}

@@ -1,0 +1,151 @@
+from concourse.bass import DstId, RemoteDMATransfer
+from concourse.mybir import AluOpType
+
+N = 4
+TK = 512
+NBANK = 8
+MAXU, MAXR, MAXT, MAXP = 8, 8, 12, 4
+
+FIRST_PIECES = [TK]
+LAST_TILES = [TK // 2, TK // 2]
+
+SCRATCH = {
+    "f1s": ("sbuf", [128, 128], "bfloat16"),
+    "f2s": ("sbuf", [128, 128], "bfloat16"),
+    "xs": ("sbuf", [128, N * TK], "bfloat16"),
+    "ts": ("sbuf", [128, N * TK], "bfloat16"),
+    "us": ("sbuf", [128, N * TK], "bfloat16"),
+    "land": ("sbuf", [128, (N - 1) * TK], "bfloat16"),
+    "ys": ("sbuf", [128, N * TK], "bfloat16"),
+}
+for _b in range(NBANK):
+    SCRATCH["ps%d" % _b] = ("psum", [128, TK], "float32")
+
+SEMAPHORES = (["ldf1", "ldf2", "sent"]
+              + ["ldx%d" % i for i in range(MAXR)] + ["ldt%d" % i for i in range(MAXR)]
+              + ["m1_%d" % i for i in range(MAXU)] + ["u_%d" % i for i in range(MAXU)]
+              + ["arr%d_%d" % (s, p) for s in range(N - 1) for p in range(MAXP)]
+              + ["m2_%d" % i for i in range(MAXT)] + ["cp_%d" % i for i in range(MAXT)]
+              + ["st_%d" % i for i in range(MAXT)])
+
+
+def _same_chip(topo, a, b):
+    return topo.host(a) == topo.host(b) and topo.chip(a) == topo.chip(b)
+
+
+def _engines(mask):
+    return bin(mask).count("1")
+
+
+def _slot(src, dst):
+    return (src - dst) % N - 1
+
+
+def _plan(cores, r, topo):
+    me = cores[r]
+    near = [j for j in range(N) if j != r and _same_chip(topo, me, cores[j])]
+    far = [j for j in range(N) if j != r and not _same_chip(topo, me, cores[j])]
+    far.sort(key=lambda j: (topo.die(cores[j]) == topo.die(me), j))
+    far_mask = topo.mask(me, cores[far[0]])
+    for j in far:
+        far_mask &= topo.mask(me, cores[j])
+    near_mask = topo.mask(me, cores[near[0]]) & ~far_mask
+    calls, off = [], 0
+    for w in FIRST_PIECES:
+        calls.append([(far[0], off, w, far_mask)])
+        off += w
+    calls.append([(far[1], 0, TK, far_mask), (near[0], 0, TK, near_mask)])
+    return calls
+
+
+def rank_program(g, core, T, topo):
+    r = T.rank_of(core)
+    if r is None:
+        return
+    cores, S = T.cores, T.sem
+    tq, vq = g.tensor, g.vector
+    calls = _plan(cores, r, topo)
+
+    units = [(j * TK + off, w) for call in calls for (j, off, w, _m) in call] + [(r * TK, TK)]
+
+    g.sync.dma_start(T.f1s[:], T.f1[:]).then_inc(S.ldf1, 16)
+    for i, (c0, w) in enumerate(units):
+        if i == len(units) - 1:
+            g.scalar.dma_start(T.f2s[:], T.f2[:]).then_inc(S.ldf2, 16)
+        g.scalar.dma_start(T.xs[:, c0:c0 + w], T.x[:, c0:c0 + w]).then_inc(S["ldx%d" % i], 16)
+        g.sync.dma_start(T.ts[:, c0:c0 + w], T.t[:, c0:c0 + w]).then_inc(S["ldt%d" % i], 16)
+
+    bank_reader = [None] * NBANK
+    n_tiles = [0]
+
+    def take_bank(reader_sem):
+        b = n_tiles[0] % NBANK
+        n_tiles[0] += 1
+        if bank_reader[b] is not None:
+            tq.wait_ge(bank_reader[b], 1)
+        bank_reader[b] = reader_sem
+        return T["ps%d" % b]
+
+    tq.wait_ge(S.ldf1, 16)
+    for i, (c0, w) in enumerate(units):
+        ps = take_bank(S["u_%d" % i])
+        tq.wait_ge(S["ldx%d" % i], 16)
+        tq.matmul(ps[:, 0:w], T.f1s[:], T.xs[:, c0:c0 + w], start=True, stop=True).then_inc(S["m1_%d" % i], 1)
+        vq.wait_ge(S["m1_%d" % i], 1)
+        vq.wait_ge(S["ldt%d" % i], 16)
+        vq.tensor_tensor(T.us[:, c0:c0 + w], ps[:, 0:w], T.ts[:, c0:c0 + w], AluOpType.mult).then_inc(S["u_%d" % i], 1)
+
+    sent, i, n_piece = 0, 0, {}
+    for call in calls:
+        transfers = []
+        for (j, off, w, mask) in call:
+            g.wait_ge(S["u_%d" % i], 1)
+            i += 1
+            p = n_piece.get(j, 0)
+            n_piece[j] = p + 1
+            s = _slot(r, j)
+            rid, pid = topo.addr(cores[j], core)
+            transfers.append(RemoteDMATransfer(
+                dst_ids=[DstId(rid=rid, pnc=pid)], dma_engine_mask=mask, remote_sem=S["arr%d_%d" % (s, p)],
+                src=T.us[:, j * TK + off:j * TK + off + w], dst=T.land[:, s * TK + off:s * TK + off + w]))
+            sent += _engines(mask)
+        g.remote_dma_fused(transfers, local_sem=S.sent)
+
+    arrivals = []
+    for j in range(N):
+        if j == r:
+            continue
+        p = 0
+        for ci, call in enumerate(_plan(cores, j, topo)):
+            for (d, off, w, mask) in call:
+                if d == r:
+                    arrivals.append((ci, 0 if _same_chip(topo, core, cores[j]) else 1, j, off, w, _engines(mask), p))
+                    p += 1
+    arrivals.sort()
+
+    tiles = [(None, 0, T.us, r * TK, r * TK, TK)]
+    for k, (_ci, _o, j, off, w, n_eng, p) in enumerate(arrivals):
+        s = _slot(j, r)
+        widths = LAST_TILES if (k == len(arrivals) - 1 and sum(LAST_TILES) == w) else [w]
+        o = off
+        for ww in widths:
+            tiles.append((S["arr%d_%d" % (s, p)], n_eng, T.land, s * TK + o, j * TK + o, ww))
+            o += ww
+
+    tq.wait_ge(S.ldf2, 16)
+    tq.wait_ge(S["u_%d" % (len(units) - 1)], 1)
+    store_q = [g.sync, g.scalar]
+    for k, (sem, cnt, buf, cb, cy, w) in enumerate(tiles):
+        ps = take_bank(S["cp_%d" % k])
+        if sem is not None:
+            tq.wait_ge(sem, cnt)
+        tq.matmul(ps[:, 0:w], T.f2s[:], buf[:, cb:cb + w], start=True, stop=True).then_inc(S["m2_%d" % k], 1)
+        vq.wait_ge(S["m2_%d" % k], 1)
+        vq.tensor_copy(T.ys[:, cy:cy + w], ps[:, 0:w]).then_inc(S["cp_%d" % k], 1)
+        q = store_q[(len(tiles) - 1 - k) % 2]
+        q.wait_ge(S["cp_%d" % k], 1)
+        q.dma_start(T.y[:, cy:cy + w], T.ys[:, cy:cy + w]).then_inc(S["st_%d" % k], 16)
+
+    for k in range(len(tiles)):
+        store_q[(len(tiles) - 1 - k) % 2].wait_ge(S["st_%d" % k], 16)
+    g.wait_ge(S.sent, sent)

@@ -4,9 +4,9 @@ from concourse.mybir import AluOpType
 N = 4
 TK = 512
 NBANK = 8
-MAXU, MAXR, MAXT, MAXP = 8, 8, 12, 4
+MAXU, MAXT, MAXP = 8, 12, 4
 
-FIRST_PIECES = [TK]
+FIRST_PIECES = [TK // 4, 3 * TK // 4]
 LAST_TILES = [TK // 2, TK // 2]
 
 SCRATCH = {
@@ -22,7 +22,7 @@ for _b in range(NBANK):
     SCRATCH["ps%d" % _b] = ("psum", [128, TK], "float32")
 
 SEMAPHORES = (["ldf1", "ldf2", "sent"]
-              + ["ldx%d" % i for i in range(MAXR)] + ["ldt%d" % i for i in range(MAXR)]
+              + ["ldx%d" % i for i in range(MAXU)] + ["ldt%d" % i for i in range(MAXU)]
               + ["m1_%d" % i for i in range(MAXU)] + ["u_%d" % i for i in range(MAXU)]
               + ["arr%d_%d" % (s, p) for s in range(N - 1) for p in range(MAXP)]
               + ["m2_%d" % i for i in range(MAXT)] + ["cp_%d" % i for i in range(MAXT)]
@@ -111,34 +111,35 @@ def rank_program(g, core, T, topo):
             sent += _engines(mask)
         g.remote_dma_fused(transfers, local_sem=S.sent)
 
-    arrivals = []
+    senders = []
     for j in range(N):
         if j == r:
             continue
-        p = 0
+        pieces, last = [], 0
         for ci, call in enumerate(_plan(cores, j, topo)):
             for (d, off, w, mask) in call:
                 if d == r:
-                    arrivals.append((ci, 0 if _same_chip(topo, core, cores[j]) else 1, j, off, w, _engines(mask), p))
-                    p += 1
-    arrivals.sort()
+                    pieces.append((off, w, S["arr%d_%d" % (_slot(j, r), len(pieces))], _engines(mask)))
+                    last = ci
+        senders.append((last, 0 if _same_chip(topo, core, cores[j]) else 1, j, pieces))
+    senders.sort(key=lambda e: e[0:3])
 
-    tiles = [(None, 0, T.us, r * TK, r * TK, TK)]
-    for k, (_ci, _o, j, off, w, n_eng, p) in enumerate(arrivals):
+    tiles = [([], T.us, r * TK, r * TK, TK)]
+    for k, (_l, _o, j, pieces) in enumerate(senders):
         s = _slot(j, r)
-        widths = LAST_TILES if (k == len(arrivals) - 1 and sum(LAST_TILES) == w) else [w]
-        o = off
-        for ww in widths:
-            tiles.append((S["arr%d_%d" % (s, p)], n_eng, T.land, s * TK + o, j * TK + o, ww))
-            o += ww
+        waits = [(sem, n) for (_off, _w, sem, n) in pieces]
+        o = 0
+        for w in (LAST_TILES if k == len(senders) - 1 else [TK]):
+            tiles.append((waits, T.land, s * TK + o, j * TK + o, w))
+            o += w
 
     tq.wait_ge(S.ldf2, 16)
     tq.wait_ge(S["u_%d" % (len(units) - 1)], 1)
     store_q = [g.sync, g.scalar]
-    for k, (sem, cnt, buf, cb, cy, w) in enumerate(tiles):
+    for k, (waits, buf, cb, cy, w) in enumerate(tiles):
         ps = take_bank(S["cp_%d" % k])
-        if sem is not None:
-            tq.wait_ge(sem, cnt)
+        for (sem, n) in waits:
+            tq.wait_ge(sem, n)
         tq.matmul(ps[:, 0:w], T.f2s[:], buf[:, cb:cb + w], start=True, stop=True).then_inc(S["m2_%d" % k], 1)
         vq.wait_ge(S["m2_%d" % k], 1)
         vq.tensor_copy(T.ys[:, cy:cy + w], ps[:, 0:w]).then_inc(S["cp_%d" % k], 1)

from concourse.bass import DstId, RemoteDMATransfer
from concourse.mybir import AluOpType

N = 4
TK = 512
NBANK = 8
MAXU, MAXT, MAXP = 8, 12, 4

FIRST_PIECES = [TK // 4, 3 * TK // 4]
LAST_TILES = [TK // 2, TK // 2]

SCRATCH = {
    "f1s": ("sbuf", [128, 128], "bfloat16"),
    "f2s": ("sbuf", [128, 128], "bfloat16"),
    "xs": ("sbuf", [128, N * TK], "bfloat16"),
    "ts": ("sbuf", [128, N * TK], "bfloat16"),
    "us": ("sbuf", [128, N * TK], "bfloat16"),
    "land": ("sbuf", [128, (N - 1) * TK], "bfloat16"),
    "ys": ("sbuf", [128, N * TK], "bfloat16"),
}
for _b in range(NBANK):
    SCRATCH["ps%d" % _b] = ("psum", [128, TK], "float32")

SEMAPHORES = (["ldf1", "ldf2", "sent"]
              + ["ldx%d" % i for i in range(MAXU)] + ["ldt%d" % i for i in range(MAXU)]
              + ["m1_%d" % i for i in range(MAXU)] + ["u_%d" % i for i in range(MAXU)]
              + ["arr%d_%d" % (s, p) for s in range(N - 1) for p in range(MAXP)]
              + ["m2_%d" % i for i in range(MAXT)] + ["cp_%d" % i for i in range(MAXT)]
              + ["st_%d" % i for i in range(MAXT)])


def _same_chip(topo, a, b):
    return topo.host(a) == topo.host(b) and topo.chip(a) == topo.chip(b)


def _engines(mask):
    return bin(mask).count("1")


def _slot(src, dst):
    return (src - dst) % N - 1


def _plan(cores, r, topo):
    me = cores[r]
    near = [j for j in range(N) if j != r and _same_chip(topo, me, cores[j])]
    far = [j for j in range(N) if j != r and not _same_chip(topo, me, cores[j])]
    far.sort(key=lambda j: (topo.die(cores[j]) == topo.die(me), j))
    far_mask = topo.mask(me, cores[far[0]])
    for j in far:
        far_mask &= topo.mask(me, cores[j])
    near_mask = topo.mask(me, cores[near[0]]) & ~far_mask
    calls, off = [], 0
    for w in FIRST_PIECES:
        calls.append([(far[0], off, w, far_mask)])
        off += w
    calls.append([(far[1], 0, TK, far_mask), (near[0], 0, TK, near_mask)])
    return calls


def rank_program(g, core, T, topo):
    r = T.rank_of(core)
    if r is None:
        return
    cores, S = T.cores, T.sem
    tq, vq = g.tensor, g.vector
    calls = _plan(cores, r, topo)

    units = [(j * TK + off, w) for call in calls for (j, off, w, _m) in call] + [(r * TK, TK)]

    g.sync.dma_start(T.f1s[:], T.f1[:]).then_inc(S.ldf1, 16)
    for i, (c0, w) in enumerate(units):
        if i == len(units) - 1:
            g.scalar.dma_start(T.f2s[:], T.f2[:]).then_inc(S.ldf2, 16)
        g.scalar.dma_start(T.xs[:, c0:c0 + w], T.x[:, c0:c0 + w]).then_inc(S["ldx%d" % i], 16)
        g.sync.dma_start(T.ts[:, c0:c0 + w], T.t[:, c0:c0 + w]).then_inc(S["ldt%d" % i], 16)

    bank_reader = [None] * NBANK
    n_tiles = [0]

    def take_bank(reader_sem):
        b = n_tiles[0] % NBANK
        n_tiles[0] += 1
        if bank_reader[b] is not None:
            tq.wait_ge(bank_reader[b], 1)
        bank_reader[b] = reader_sem
        return T["ps%d" % b]

    tq.wait_ge(S.ldf1, 16)
    for i, (c0, w) in enumerate(units):
        ps = take_bank(S["u_%d" % i])
        tq.wait_ge(S["ldx%d" % i], 16)
        tq.matmul(ps[:, 0:w], T.f1s[:], T.xs[:, c0:c0 + w], start=True, stop=True).then_inc(S["m1_%d" % i], 1)
        vq.wait_ge(S["m1_%d" % i], 1)
        vq.wait_ge(S["ldt%d" % i], 16)
        vq.tensor_tensor(T.us[:, c0:c0 + w], ps[:, 0:w], T.ts[:, c0:c0 + w], AluOpType.mult).then_inc(S["u_%d" % i], 1)

    sent, i, n_piece = 0, 0, {}
    for call in calls:
        transfers = []
        for (j, off, w, mask) in call:
            g.wait_ge(S["u_%d" % i], 1)
            i += 1
            p = n_piece.get(j, 0)
            n_piece[j] = p + 1
            s = _slot(r, j)
            rid, pid = topo.addr(cores[j], core)
            transfers.append(RemoteDMATransfer(
                dst_ids=[DstId(rid=rid, pnc=pid)], dma_engine_mask=mask, remote_sem=S["arr%d_%d" % (s, p)],
                src=T.us[:, j * TK + off:j * TK + off + w], dst=T.land[:, s * TK + off:s * TK + off + w]))
            sent += _engines(mask)
        g.remote_dma_fused(transfers, local_sem=S.sent)

    senders = []
    for j in range(N):
        if j == r:
            continue
        pieces, last = [], 0
        for ci, call in enumerate(_plan(cores, j, topo)):
            for (d, off, w, mask) in call:
                if d == r:
                    pieces.append((off, w, S["arr%d_%d" % (_slot(j, r), len(pieces))], _engines(mask)))
                    last = ci
        senders.append((last, 0 if _same_chip(topo, core, cores[j]) else 1, j, pieces))
    senders.sort(key=lambda e: e[0:3])

    tiles = [([], T.us, r * TK, r * TK, TK)]
    for k, (_l, _o, j, pieces) in enumerate(senders):
        s = _slot(j, r)
        waits = [(sem, n) for (_off, _w, sem, n) in pieces]
        o = 0
        for w in (LAST_TILES if k == len(senders) - 1 else [TK]):
            tiles.append((waits, T.land, s * TK + o, j * TK + o, w))
            o += w

    tq.wait_ge(S.ldf2, 16)
    tq.wait_ge(S["u_%d" % (len(units) - 1)], 1)
    store_q = [g.sync, g.scalar]
    for k, (waits, buf, cb, cy, w) in enumerate(tiles):
        ps = take_bank(S["cp_%d" % k])
        for (sem, n) in waits:
            tq.wait_ge(sem, n)
        tq.matmul(ps[:, 0:w], T.f2s[:], buf[:, cb:cb + w], start=True, stop=True).then_inc(S["m2_%d" % k], 1)
        vq.wait_ge(S["m2_%d" % k], 1)
        vq.tensor_copy(T.ys[:, cy:cy + w], ps[:, 0:w]).then_inc(S["cp_%d" % k], 1)
        q = store_q[(len(tiles) - 1 - k) % 2]
        q.wait_ge(S["cp_%d" % k], 1)
        q.dma_start(T.y[:, cy:cy + w], T.ys[:, cy:cy + w]).then_inc(S["st_%d" % k], 16)

    for k in range(len(tiles)):
        store_q[(len(tiles) - 1 - k) % 2].wait_ge(S["st_%d" % k], 16)
    g.wait_ge(S.sent, sent)
